import numpy as np
import ml_dtypes


def mxq(x, axis, fmt="e4m3"):
    dtype, down = {"e4m3": (ml_dtypes.float8_e4m3fn, 7), "e5m2": (ml_dtypes.float8_e5m2, 14)}[fmt]
    v = np.moveaxis(np.asarray(x, np.float32).astype(ml_dtypes.bfloat16).astype(np.float64), axis, -1)
    blocks = v.reshape(v.shape[:-1] + (-1, 32))
    amax = np.abs(blocks).max(-1, keepdims=True)
    byte = np.maximum(np.where(amax > 0, np.frexp(amax)[1] - 1 + 127, 0) - down, 1)
    scale = np.exp2(byte - 127.0)
    codes = (blocks / scale).astype(np.float32).astype(dtype).astype(np.float64)
    return np.moveaxis((codes * scale).reshape(v.shape), -1, axis)


WIDE = False


def mx_kscale(k):
    if not WIDE:
        return np.ones(k)
    levels = np.array([10, -10, 5, -5, 0])
    if k % 512:
        return np.exp2(np.random.permutation(np.resize(levels, k // 32))).repeat(32)
    a = np.empty((k // 512, 16))
    for p in range(k // 512):
        a[p, :8] = np.random.permutation(np.resize(levels, 8))
        for g in range(8):
            far = levels[np.abs(levels - a[p, g]) >= 10]
            a[p, g + 8] = far[np.random.randint(len(far))]
    return np.exp2(a.ravel()).repeat(32)


def f64(x):
    return np.asarray(x).astype(np.float64)


def striped(idx):
    return np.tile(idx.reshape(-1, 16).T, (8, 1)).astype(np.uint16)


def unstriped(offs):
    return offs[:16].T.reshape(-1).astype(np.int64)


K, T, S, H, N = 1024, 1024, 512, 512, 128


def setup_inputs():
    n = np.random.standard_normal
    s = mx_kscale(K)[:, None]
    u = mx_kscale(H)
    return {
        "xT": (n((K, T)) * s).astype(np.float32),
        "w1": (n((K, N)) / np.sqrt(2 * K) / s).astype(np.float32),
        "w2": (n((K, H)) / np.sqrt(K) / s * u).astype(np.float32),
        "w3": (n((H, N)) / np.sqrt(2 * H) / u[:, None]).astype(np.float32),
        "offs": striped(np.random.permutation(T)[:S]),
    }


def reference(xT, w1, w2, w3, offs):
    xq = mxq(f64(xT)[:, unstriped(offs)], 0, "e4m3")
    h = mxq(f64(w2), 0, "e4m3").T @ xq
    return mxq(f64(w1), 0, "e4m3").T @ xq + mxq(f64(w3), 0, "e4m3").T @ mxq(h, 0, "e4m3")

@@ -1,0 +1,186 @@
+from contextlib import ExitStack
+
+import concourse.mybir as mybir
+
+K, T, S, H, N = 1024, 1024, 512, 512, 128
+FLOPS = 2 * S * (K * H + K * N + H * N)
+
+F32 = mybir.dt.float32
+BF16 = mybir.dt.bfloat16
+U32 = mybir.dt.uint32
+I32 = mybir.dt.int32
+U16 = mybir.dt.uint16
+U8 = mybir.dt.uint8
+FP8X4 = mybir.dt.float8_e4m3fn_x4
+
+P = 128
+PACK = 4
+K_PASS = P * PACK
+PASSES = K // K_PASS
+CHUNK = 128
+CHUNKS = S // CHUNK
+
+X_WIDTHS = ((512, 512), (256, 256, 256, 256))
+X_VECTOR_COLS = ((304, 304), (0, 0, 64, 112))
+W2_VECTOR_M = (30, 28)
+W2_PIECES = 2
+
+
+def tile_picked_lora_none_e_kernel(tc, xT, w1, w2, w3, offs, out):
+    nc = tc.nc
+    with ExitStack() as ctx:
+        keep = ctx.enter_context(tc.tile_pool(name="keep", bufs=1))
+        psum = ctx.enter_context(tc.psum_pool(name="psum", bufs=1))
+
+        def rows(w, z):
+            return w[z * K_PASS : (z + 1) * K_PASS, :].rearrange("(p j) c -> p j c", j=PACK)
+
+        def mx_tiles(name, width):
+            codes = keep.tile([P, width], U32, name=name + "_codes", align_bytes=64)
+            scales = keep.tile([P, width], U8, name=name + "_scales", align_bytes=64)
+            return codes, scales
+
+        def quantize(operand, values):
+            codes, scales = operand
+            nc.vector.quantize_mx(out=codes[:].bitcast(FP8X4), scales=scales[:], in_=values)
+
+        def matmul(acc, stationary, m_cols, moving, n_cols, start, stop):
+            nc.tensor.matmul_mx(
+                out=acc,
+                lhsT=stationary[0][:, m_cols].bitcast(FP8X4),
+                lhsT_scale=stationary[1][:, m_cols],
+                rhs=moving[0][:, n_cols].bitcast(FP8X4),
+                rhs_scale=moving[1][:, n_cols],
+                start=start,
+                stop=stop,
+            )
+
+        offsets = keep.tile([P, S // 16], U16, name="offsets")
+        x_raw = []
+        for z in range(PASSES):
+            tiles = []
+            first = 0
+            for a, width in enumerate(X_WIDTHS[z]):
+                raw = keep.tile([P, PACK, width], F32, name="x_raw%d%d" % (z, a))
+                nc.sync.dma_start(out=raw[:], in_=rows(xT, z)[:, :, first : first + width])
+                tiles.append((first, width, raw))
+                first = first + width
+                if z == 0 and a == 0:
+                    nc.sync.dma_start(offsets[:], offs)
+            x_raw.append(tiles)
+        w2_raw = []
+        for z in range(PASSES):
+            width = H // W2_PIECES
+            tiles = []
+            for a in range(W2_PIECES):
+                raw = keep.tile([P, PACK, width], F32, name="w2_raw%d%d" % (z, a))
+                nc.sync.dma_start(out=raw[:], in_=rows(w2, z)[:, :, a * width : (a + 1) * width])
+                tiles.append(raw)
+            w2_raw.append(tiles)
+        w1_raw = keep.tile([P, PASSES, PACK, N], F32, name="w1_raw")
+        nc.sync.dma_start(out=w1_raw[:], in_=w1.rearrange("(z p j) c -> p z j c", z=PASSES, j=PACK))
+        w3_raw = keep.tile([P, PACK, N], F32, name="w3_raw")
+        nc.sync.dma_start(out=w3_raw[:], in_=rows(w3, 0))
+
+        all_codes = [keep.tile([P, T], U32, name="all_codes%d" % z, align_bytes=64) for z in range(PASSES)]
+        all_scales = keep.tile([P, T], U8, name="all_scales", align_bytes=64)
+        nc.vector.memset(all_scales[:].bitcast(I32), 0)
+        x_scales = keep.tile([P, S], U8, name="x_scales", align_bytes=64)
+        x_mx = [None, None]
+
+        def quantize_tokens(z):
+            for a, (first, width, raw) in enumerate(x_raw[z]):
+                laid = keep.tile([P, width * PACK], BF16, name="x_laid%d%d" % (z, a), align_bytes=64)
+                dst = laid[:].rearrange("p (c i j) -> p c j i", i=4, j=PACK)
+                src = raw[:].rearrange("p j (c i) -> p c j i", i=4)
+                cut = X_VECTOR_COLS[z][a] // 4
+                nc.scalar.copy(out=dst[:, cut:], in_=src[:, cut:])
+                if cut:
+                    nc.vector.tensor_copy(out=dst[:, :cut], in_=src[:, :cut])
+                cols = slice(first, first + width)
+                nc.vector.quantize_mx(
+                    out=all_codes[z][:, cols].bitcast(FP8X4), scales=all_scales[4 * z :, cols], in_=laid[:]
+                )
+
+        def pick_codes(z, tag):
+            codes = keep.tile([P, S], U32, name="x_codes%d" % z, tag=tag, align_bytes=64)
+            nc.vector.tensor_copy(out=codes[:], in_=all_codes[z][:].indirect(offsets[:]))
+            x_mx[z] = (codes, x_scales[4 * z :, :])
+
+        def pick_scales():
+            nc.vector.tensor_copy(out=x_scales[:], in_=all_scales[:].indirect(offsets[:]))
+
+        w2_mx = [mx_tiles("w2%d" % z, H) for z in range(PASSES)]
+
+        def prepare_w2(z):
+            dealt = keep.tile([P, H * PACK], BF16, name="w2_dealt%d" % z, tag="dealt%d" % z, align_bytes=64)
+            whole = dealt[:].rearrange("p (t m j) -> p m j t", t=PACK, j=PACK)
+            width = P // W2_PIECES
+            for a, raw in enumerate(w2_raw[z]):
+                dst = whole[:, a * width : (a + 1) * width]
+                src = raw[:].rearrange("p j (m t) -> p m j t", t=PACK)
+                cut = W2_VECTOR_M[z] if a == W2_PIECES - 1 else 0
+                nc.scalar.copy(out=dst[:, cut:], in_=src[:, cut:])
+                if cut:
+                    nc.vector.tensor_copy(out=dst[:, :cut], in_=src[:, :cut])
+            quantize(w2_mx[z], dealt[:])
+
+        h_banks = [psum.tile([P, PACK, CHUNK], F32, name="h_bank%d" % c) for c in range(CHUNKS)]
+        out_banks = [psum.tile([P, CHUNK], F32, name="out_bank%d" % c) for c in range(CHUNKS)]
+
+        def hidden_pass(z):
+            for c in range(CHUNKS):
+                for t in range(PACK):
+                    matmul(
+                        h_banks[c][:, t, :], w2_mx[z], slice(t * P, (t + 1) * P),
+                        x_mx[z], slice(c * CHUNK, (c + 1) * CHUNK),
+                        start=(z == 0 and t == 0), stop=(z == PASSES - 1 and t == PACK - 1),
+                    )
+
+        quantize_tokens(0)
+        pick_codes(0, "x_codes0")
+        quantize_tokens(1)
+        pick_scales()
+        prepare_w2(0)
+        pick_codes(1, "dealt0")
+        hidden_pass(0)
+        prepare_w2(1)
+        hidden_pass(1)
+
+        w1_laid = keep.tile([P, PASSES * N * PACK], BF16, name="w1_laid", align_bytes=64)
+        for z in range(PASSES):
+            copy = nc.scalar.copy if z == 0 else nc.vector.tensor_copy
+            copy(
+                out=w1_laid[:, z * N * PACK : (z + 1) * N * PACK].rearrange("p (c i j) -> p c j i", i=4, j=PACK),
+                in_=w1_raw[:, z].rearrange("p j (c i) -> p c j i", i=4),
+            )
+        w3_laid = keep.tile([P, N * PACK], BF16, name="w3_laid", align_bytes=64)
+        nc.vector.tensor_copy(
+            out=w3_laid[:].rearrange("p (c i j) -> p c j i", i=4, j=PACK),
+            in_=w3_raw[:].rearrange("p j (c i) -> p c j i", i=4),
+        )
+        w1_mx = mx_tiles("w1", PASSES * N)
+        quantize(w1_mx, w1_laid[:])
+        w3_mx = mx_tiles("w3", N)
+        quantize(w3_mx, w3_laid[:])
+
+        for c in range(CHUNKS):
+            for z in range(PASSES):
+                matmul(
+                    out_banks[c][:], w1_mx, slice(z * N, (z + 1) * N),
+                    x_mx[z], slice(c * CHUNK, (c + 1) * CHUNK), start=(z == 0), stop=False,
+                )
+
+        for c in range(CHUNKS):
+            h_laid = keep.tile([P, CHUNK, PACK], BF16, name="h_laid%d" % c, align_bytes=64)
+            src = h_banks[c][:].rearrange("p t n -> p n t")
+            if c < CHUNKS - 1:
+                nc.scalar.copy(out=h_laid[:], in_=src)
+            else:
+                nc.vector.tensor_copy(out=h_laid[:], in_=src)
+            h_mx = mx_tiles("h%d" % c, CHUNK)
+            quantize(h_mx, h_laid[:].rearrange("p n t -> p (n t)"))
+            matmul(out_banks[c][:], w3_mx, slice(0, N), h_mx, slice(0, CHUNK), start=False, stop=True)
+            result = keep.tile([P, CHUNK], F32, name="result%d" % c)
+            nc.scalar.copy(out=result[:], in_=out_banks[c][:])
+            nc.sync.dma_start(out=out[:, c * CHUNK : (c + 1) * CHUNK], in_=result[:])

@@ -20,9 +20,9 @@ PASSES = K // K_PASS
 CHUNK = 128
 CHUNKS = S // CHUNK
 
-X_WIDTHS = ((512, 512), (256, 256, 256, 256))
-X_VECTOR_COLS = ((304, 304), (0, 0, 64, 112))
-W2_VECTOR_M = (30, 28)
+X_WIDTHS = ((512, 256, 256), (256, 256, 256, 256))
+X_VECTOR_COLS = ((304, 96, 112), (0, 80, 104, 112))
+W2_VECTOR_M = (0, 30)
 W2_PIECES = 2
 
 
@@ -77,8 +77,11 @@ def tile_picked_lora_none_e_kernel(tc, xT, w1, w2, w3, offs, out):
                 nc.sync.dma_start(out=raw[:], in_=rows(w2, z)[:, :, a * width : (a + 1) * width])
                 tiles.append(raw)
             w2_raw.append(tiles)
-        w1_raw = keep.tile([P, PASSES, PACK, N], F32, name="w1_raw")
-        nc.sync.dma_start(out=w1_raw[:], in_=w1.rearrange("(z p j) c -> p z j c", z=PASSES, j=PACK))
+        w1_raw = []
+        for z in range(PASSES):
+            raw = keep.tile([P, PACK, N], F32, name="w1_raw%d" % z)
+            nc.sync.dma_start(out=raw[:], in_=rows(w1, z))
+            w1_raw.append(raw)
         w3_raw = keep.tile([P, PACK, N], F32, name="w3_raw")
         nc.sync.dma_start(out=w3_raw[:], in_=rows(w3, 0))
 
@@ -113,7 +116,7 @@ def tile_picked_lora_none_e_kernel(tc, xT, w1, w2, w3, offs, out):
         w2_mx = [mx_tiles("w2%d" % z, H) for z in range(PASSES)]
 
         def prepare_w2(z):
-            dealt = keep.tile([P, H * PACK], BF16, name="w2_dealt%d" % z, tag="dealt%d" % z, align_bytes=64)
+            dealt = keep.tile([P, H * PACK], BF16, name="w2_dealt%d" % z, align_bytes=64)
             whole = dealt[:].rearrange("p (t m j) -> p m j t", t=PACK, j=PACK)
             width = P // W2_PIECES
             for a, raw in enumerate(w2_raw[z]):
@@ -126,7 +129,6 @@ def tile_picked_lora_none_e_kernel(tc, xT, w1, w2, w3, offs, out):
             quantize(w2_mx[z], dealt[:])
 
         h_banks = [psum.tile([P, PACK, CHUNK], F32, name="h_bank%d" % c) for c in range(CHUNKS)]
-        out_banks = [psum.tile([P, CHUNK], F32, name="out_bank%d" % c) for c in range(CHUNKS)]
 
         def hidden_pass(z):
             for c in range(CHUNKS):
@@ -141,26 +143,29 @@ def tile_picked_lora_none_e_kernel(tc, xT, w1, w2, w3, offs, out):
         pick_codes(0, "x_codes0")
         quantize_tokens(1)
         pick_scales()
+        pick_codes(1, "x_codes1")
+        warm = psum.tile([P, S], F32, name="warm", tag="out_bank0")
+        for width in (512, 512, 256):
+            matmul(warm[:, :width], x_mx[0], slice(0, P), x_mx[0], slice(0, width), start=True, stop=True)
+        out_banks = [psum.tile([P, CHUNK], F32, name="out_bank%d" % c, tag="out_bank%d" % c) for c in range(CHUNKS)]
         prepare_w2(0)
-        pick_codes(1, "dealt0")
         hidden_pass(0)
         prepare_w2(1)
         hidden_pass(1)
 
         w1_laid = keep.tile([P, PASSES * N * PACK], BF16, name="w1_laid", align_bytes=64)
         for z in range(PASSES):
-            copy = nc.scalar.copy if z == 0 else nc.vector.tensor_copy
-            copy(
+            nc.scalar.copy(
                 out=w1_laid[:, z * N * PACK : (z + 1) * N * PACK].rearrange("p (c i j) -> p c j i", i=4, j=PACK),
-                in_=w1_raw[:, z].rearrange("p j (c i) -> p c j i", i=4),
+                in_=w1_raw[z][:].rearrange("p j (c i) -> p c j i", i=4),
             )
+        w1_mx = mx_tiles("w1", PASSES * N)
+        quantize(w1_mx, w1_laid[:])
         w3_laid = keep.tile([P, N * PACK], BF16, name="w3_laid", align_bytes=64)
         nc.vector.tensor_copy(
             out=w3_laid[:].rearrange("p (c i j) -> p c j i", i=4, j=PACK),
             in_=w3_raw[:].rearrange("p j (c i) -> p c j i", i=4),
         )
-        w1_mx = mx_tiles("w1", PASSES * N)
-        quantize(w1_mx, w1_laid[:])
         w3_mx = mx_tiles("w3", N)
         quantize(w3_mx, w3_laid[:])
 
@@ -171,16 +176,22 @@ def tile_picked_lora_none_e_kernel(tc, xT, w1, w2, w3, offs, out):
                     x_mx[z], slice(c * CHUNK, (c + 1) * CHUNK), start=(z == 0), stop=False,
                 )
 
+        h_all = []
         for c in range(CHUNKS):
             h_laid = keep.tile([P, CHUNK, PACK], BF16, name="h_laid%d" % c, align_bytes=64)
             src = h_banks[c][:].rearrange("p t n -> p n t")
-            if c < CHUNKS - 1:
+            if c != 2:
                 nc.scalar.copy(out=h_laid[:], in_=src)
             else:
                 nc.vector.tensor_copy(out=h_laid[:], in_=src)
             h_mx = mx_tiles("h%d" % c, CHUNK)
             quantize(h_mx, h_laid[:].rearrange("p n t -> p (n t)"))
+            h_all.append(h_mx)
             matmul(out_banks[c][:], w3_mx, slice(0, N), h_mx, slice(0, CHUNK), start=False, stop=True)
+        for c in range(CHUNKS):
             result = keep.tile([P, CHUNK], F32, name="result%d" % c)
-            nc.scalar.copy(out=result[:], in_=out_banks[c][:])
+            if c < CHUNKS - 1:
+                nc.scalar.copy(out=result[:], in_=out_banks[c][:])
+            else:
+                nc.vector.tensor_copy(out=result[:], in_=out_banks[c][:])
             nc.sync.dma_start(out=out[:, c * CHUNK : (c + 1) * CHUNK], in_=result[:])

@@ -20,9 +20,9 @@ PASSES = K // K_PASS
 CHUNK = 128
 CHUNKS = S // CHUNK
 
-X_WIDTHS = ((512, 256, 256), (256, 256, 256, 256))
-X_VECTOR_COLS = ((304, 96, 112), (0, 80, 104, 112))
-W2_VECTOR_M = (0, 30)
+X_WIDTHS = ((512, 512), (256, 256, 256, 256))
+X_VECTOR_COLS = ((320, 320), (0, 0, 96, 128))
+W2_VECTOR_M = ((0, 0), (24, 34))
 W2_PIECES = 2
 
 
@@ -77,11 +77,8 @@ def tile_picked_lora_none_e_kernel(tc, xT, w1, w2, w3, offs, out):
                 nc.sync.dma_start(out=raw[:], in_=rows(w2, z)[:, :, a * width : (a + 1) * width])
                 tiles.append(raw)
             w2_raw.append(tiles)
-        w1_raw = []
-        for z in range(PASSES):
-            raw = keep.tile([P, PACK, N], F32, name="w1_raw%d" % z)
-            nc.sync.dma_start(out=raw[:], in_=rows(w1, z))
-            w1_raw.append(raw)
+        w1_raw = keep.tile([P, PASSES, PACK, N], F32, name="w1_raw")
+        nc.sync.dma_start(out=w1_raw[:], in_=w1.rearrange("(z p j) c -> p z j c", z=PASSES, j=PACK))
         w3_raw = keep.tile([P, PACK, N], F32, name="w3_raw")
         nc.sync.dma_start(out=w3_raw[:], in_=rows(w3, 0))
 
@@ -122,7 +119,7 @@ def tile_picked_lora_none_e_kernel(tc, xT, w1, w2, w3, offs, out):
             for a, raw in enumerate(w2_raw[z]):
                 dst = whole[:, a * width : (a + 1) * width]
                 src = raw[:].rearrange("p j (m t) -> p m j t", t=PACK)
-                cut = W2_VECTOR_M[z] if a == W2_PIECES - 1 else 0
+                cut = W2_VECTOR_M[z][a]
                 nc.scalar.copy(out=dst[:, cut:], in_=src[:, cut:])
                 if cut:
                     nc.vector.tensor_copy(out=dst[:, :cut], in_=src[:, :cut])
@@ -155,9 +152,10 @@ def tile_picked_lora_none_e_kernel(tc, xT, w1, w2, w3, offs, out):
 
         w1_laid = keep.tile([P, PASSES * N * PACK], BF16, name="w1_laid", align_bytes=64)
         for z in range(PASSES):
-            nc.scalar.copy(
+            copy = nc.scalar.copy if z == 0 else nc.vector.tensor_copy
+            copy(
                 out=w1_laid[:, z * N * PACK : (z + 1) * N * PACK].rearrange("p (c i j) -> p c j i", i=4, j=PACK),
-                in_=w1_raw[z][:].rearrange("p j (c i) -> p c j i", i=4),
+                in_=w1_raw[:, z].rearrange("p j (c i) -> p c j i", i=4),
             )
         w1_mx = mx_tiles("w1", PASSES * N)
         quantize(w1_mx, w1_laid[:])

@@ -21,8 +21,8 @@ CHUNK = 128
 CHUNKS = S // CHUNK
 
 X_WIDTHS = ((512, 512), (256, 256, 256, 256))
-X_VECTOR_COLS = ((320, 320), (0, 0, 96, 128))
-W2_VECTOR_M = ((0, 0), (24, 34))
+X_VECTOR_COLS = ((320, 320), (0, 0, 0, 176))
+W2_VECTOR_M = ((0, 0), (0, 36))
 W2_PIECES = 2
 
 
@@ -141,9 +141,6 @@ def tile_picked_lora_none_e_kernel(tc, xT, w1, w2, w3, offs, out):
         quantize_tokens(1)
         pick_scales()
         pick_codes(1, "x_codes1")
-        warm = psum.tile([P, S], F32, name="warm", tag="out_bank0")
-        for width in (512, 512, 256):
-            matmul(warm[:, :width], x_mx[0], slice(0, P), x_mx[0], slice(0, width), start=True, stop=True)
         out_banks = [psum.tile([P, CHUNK], F32, name="out_bank%d" % c, tag="out_bank%d" % c) for c in range(CHUNKS)]
         prepare_w2(0)
         hidden_pass(0)
@@ -186,10 +183,10 @@ def tile_picked_lora_none_e_kernel(tc, xT, w1, w2, w3, offs, out):
             quantize(h_mx, h_laid[:].rearrange("p n t -> p (n t)"))
             h_all.append(h_mx)
             matmul(out_banks[c][:], w3_mx, slice(0, N), h_mx, slice(0, CHUNK), start=False, stop=True)
+        results = [keep.tile([P, 2 * CHUNK], F32, name="result%d" % half) for half in range(2)]
         for c in range(CHUNKS):
-            result = keep.tile([P, CHUNK], F32, name="result%d" % c)
-            if c < CHUNKS - 1:
-                nc.scalar.copy(out=result[:], in_=out_banks[c][:])
-            else:
-                nc.vector.tensor_copy(out=result[:], in_=out_banks[c][:])
-            nc.sync.dma_start(out=out[:, c * CHUNK : (c + 1) * CHUNK], in_=result[:])
+            half, e = divmod(c, 2)
+            copy = nc.vector.tensor_copy if c == CHUNKS - 1 else nc.scalar.copy
+            copy(out=results[half][:, e * CHUNK : (e + 1) * CHUNK], in_=out_banks[c][:])
+        for half in range(2):
+            nc.sync.dma_start(out=out[:, 2 * CHUNK * half : 2 * CHUNK * (half + 1)], in_=results[half][:])

from contextlib import ExitStack

import concourse.mybir as mybir

K, T, S, H, N = 1024, 1024, 512, 512, 128
FLOPS = 2 * S * (K * H + K * N + H * N)

F32 = mybir.dt.float32
BF16 = mybir.dt.bfloat16
U32 = mybir.dt.uint32
I32 = mybir.dt.int32
U16 = mybir.dt.uint16
U8 = mybir.dt.uint8
FP8X4 = mybir.dt.float8_e4m3fn_x4

P = 128
PACK = 4
K_PASS = P * PACK
PASSES = K // K_PASS
CHUNK = 128
CHUNKS = S // CHUNK

X_WIDTHS = ((512, 512), (256, 256, 256, 256))
X_VECTOR_COLS = ((320, 320), (0, 0, 0, 176))
W2_VECTOR_M = ((0, 0), (0, 36))
W2_PIECES = 2


def tile_picked_lora_none_e_kernel(tc, xT, w1, w2, w3, offs, out):
    nc = tc.nc
    with ExitStack() as ctx:
        keep = ctx.enter_context(tc.tile_pool(name="keep", bufs=1))
        psum = ctx.enter_context(tc.psum_pool(name="psum", bufs=1))

        def rows(w, z):
            return w[z * K_PASS : (z + 1) * K_PASS, :].rearrange("(p j) c -> p j c", j=PACK)

        def mx_tiles(name, width):
            codes = keep.tile([P, width], U32, name=name + "_codes", align_bytes=64)
            scales = keep.tile([P, width], U8, name=name + "_scales", align_bytes=64)
            return codes, scales

        def quantize(operand, values):
            codes, scales = operand
            nc.vector.quantize_mx(out=codes[:].bitcast(FP8X4), scales=scales[:], in_=values)

        def matmul(acc, stationary, m_cols, moving, n_cols, start, stop):
            nc.tensor.matmul_mx(
                out=acc,
                lhsT=stationary[0][:, m_cols].bitcast(FP8X4),
                lhsT_scale=stationary[1][:, m_cols],
                rhs=moving[0][:, n_cols].bitcast(FP8X4),
                rhs_scale=moving[1][:, n_cols],
                start=start,
                stop=stop,
            )

        offsets = keep.tile([P, S // 16], U16, name="offsets")
        x_raw = []
        for z in range(PASSES):
            tiles = []
            first = 0
            for a, width in enumerate(X_WIDTHS[z]):
                raw = keep.tile([P, PACK, width], F32, name="x_raw%d%d" % (z, a))
                nc.sync.dma_start(out=raw[:], in_=rows(xT, z)[:, :, first : first + width])
                tiles.append((first, width, raw))
                first = first + width
                if z == 0 and a == 0:
                    nc.sync.dma_start(offsets[:], offs)
            x_raw.append(tiles)
        w2_raw = []
        for z in range(PASSES):
            width = H // W2_PIECES
            tiles = []
            for a in range(W2_PIECES):
                raw = keep.tile([P, PACK, width], F32, name="w2_raw%d%d" % (z, a))
                nc.sync.dma_start(out=raw[:], in_=rows(w2, z)[:, :, a * width : (a + 1) * width])
                tiles.append(raw)
            w2_raw.append(tiles)
        w1_raw = keep.tile([P, PASSES, PACK, N], F32, name="w1_raw")
        nc.sync.dma_start(out=w1_raw[:], in_=w1.rearrange("(z p j) c -> p z j c", z=PASSES, j=PACK))
        w3_raw = keep.tile([P, PACK, N], F32, name="w3_raw")
        nc.sync.dma_start(out=w3_raw[:], in_=rows(w3, 0))

        all_codes = [keep.tile([P, T], U32, name="all_codes%d" % z, align_bytes=64) for z in range(PASSES)]
        all_scales = keep.tile([P, T], U8, name="all_scales", align_bytes=64)
        nc.vector.memset(all_scales[:].bitcast(I32), 0)
        x_scales = keep.tile([P, S], U8, name="x_scales", align_bytes=64)
        x_mx = [None, None]

        def quantize_tokens(z):
            for a, (first, width, raw) in enumerate(x_raw[z]):
                laid = keep.tile([P, width * PACK], BF16, name="x_laid%d%d" % (z, a), align_bytes=64)
                dst = laid[:].rearrange("p (c i j) -> p c j i", i=4, j=PACK)
                src = raw[:].rearrange("p j (c i) -> p c j i", i=4)
                cut = X_VECTOR_COLS[z][a] // 4
                nc.scalar.copy(out=dst[:, cut:], in_=src[:, cut:])
                if cut:
                    nc.vector.tensor_copy(out=dst[:, :cut], in_=src[:, :cut])
                cols = slice(first, first + width)
                nc.vector.quantize_mx(
                    out=all_codes[z][:, cols].bitcast(FP8X4), scales=all_scales[4 * z :, cols], in_=laid[:]
                )

        def pick_codes(z, tag):
            codes = keep.tile([P, S], U32, name="x_codes%d" % z, tag=tag, align_bytes=64)
            nc.vector.tensor_copy(out=codes[:], in_=all_codes[z][:].indirect(offsets[:]))
            x_mx[z] = (codes, x_scales[4 * z :, :])

        def pick_scales():
            nc.vector.tensor_copy(out=x_scales[:], in_=all_scales[:].indirect(offsets[:]))

        w2_mx = [mx_tiles("w2%d" % z, H) for z in range(PASSES)]

        def prepare_w2(z):
            dealt = keep.tile([P, H * PACK], BF16, name="w2_dealt%d" % z, align_bytes=64)
            whole = dealt[:].rearrange("p (t m j) -> p m j t", t=PACK, j=PACK)
            width = P // W2_PIECES
            for a, raw in enumerate(w2_raw[z]):
                dst = whole[:, a * width : (a + 1) * width]
                src = raw[:].rearrange("p j (m t) -> p m j t", t=PACK)
                cut = W2_VECTOR_M[z][a]
                nc.scalar.copy(out=dst[:, cut:], in_=src[:, cut:])
                if cut:
                    nc.vector.tensor_copy(out=dst[:, :cut], in_=src[:, :cut])
            quantize(w2_mx[z], dealt[:])

        h_banks = [psum.tile([P, PACK, CHUNK], F32, name="h_bank%d" % c) for c in range(CHUNKS)]

        def hidden_pass(z):
            for c in range(CHUNKS):
                for t in range(PACK):
                    matmul(
                        h_banks[c][:, t, :], w2_mx[z], slice(t * P, (t + 1) * P),
                        x_mx[z], slice(c * CHUNK, (c + 1) * CHUNK),
                        start=(z == 0 and t == 0), stop=(z == PASSES - 1 and t == PACK - 1),
                    )

        quantize_tokens(0)
        pick_codes(0, "x_codes0")
        quantize_tokens(1)
        pick_scales()
        pick_codes(1, "x_codes1")
        out_banks = [psum.tile([P, CHUNK], F32, name="out_bank%d" % c, tag="out_bank%d" % c) for c in range(CHUNKS)]
        prepare_w2(0)
        hidden_pass(0)
        prepare_w2(1)
        hidden_pass(1)

        w1_laid = keep.tile([P, PASSES * N * PACK], BF16, name="w1_laid", align_bytes=64)
        for z in range(PASSES):
            copy = nc.scalar.copy if z == 0 else nc.vector.tensor_copy
            copy(
                out=w1_laid[:, z * N * PACK : (z + 1) * N * PACK].rearrange("p (c i j) -> p c j i", i=4, j=PACK),
                in_=w1_raw[:, z].rearrange("p j (c i) -> p c j i", i=4),
            )
        w1_mx = mx_tiles("w1", PASSES * N)
        quantize(w1_mx, w1_laid[:])
        w3_laid = keep.tile([P, N * PACK], BF16, name="w3_laid", align_bytes=64)
        nc.vector.tensor_copy(
            out=w3_laid[:].rearrange("p (c i j) -> p c j i", i=4, j=PACK),
            in_=w3_raw[:].rearrange("p j (c i) -> p c j i", i=4),
        )
        w3_mx = mx_tiles("w3", N)
        quantize(w3_mx, w3_laid[:])

        for c in range(CHUNKS):
            for z in range(PASSES):
                matmul(
                    out_banks[c][:], w1_mx, slice(z * N, (z + 1) * N),
                    x_mx[z], slice(c * CHUNK, (c + 1) * CHUNK), start=(z == 0), stop=False,
                )

        h_all = []
        for c in range(CHUNKS):
            h_laid = keep.tile([P, CHUNK, PACK], BF16, name="h_laid%d" % c, align_bytes=64)
            src = h_banks[c][:].rearrange("p t n -> p n t")
            if c != 2:
                nc.scalar.copy(out=h_laid[:], in_=src)
            else:
                nc.vector.tensor_copy(out=h_laid[:], in_=src)
            h_mx = mx_tiles("h%d" % c, CHUNK)
            quantize(h_mx, h_laid[:].rearrange("p n t -> p (n t)"))
            h_all.append(h_mx)
            matmul(out_banks[c][:], w3_mx, slice(0, N), h_mx, slice(0, CHUNK), start=False, stop=True)
        results = [keep.tile([P, 2 * CHUNK], F32, name="result%d" % half) for half in range(2)]
        for c in range(CHUNKS):
            half, e = divmod(c, 2)
            copy = nc.vector.tensor_copy if c == CHUNKS - 1 else nc.scalar.copy
            copy(out=results[half][:, e * CHUNK : (e + 1) * CHUNK], in_=out_banks[c][:])
        for half in range(2):
            nc.sync.dma_start(out=out[:, 2 * CHUNK * half : 2 * CHUNK * (half + 1)], in_=results[half][:])
